import numpy as np
import ml_dtypes


def mxq(x, axis, fmt="e4m3"):
    dtype, down = {"e4m3": (ml_dtypes.float8_e4m3fn, 7), "e5m2": (ml_dtypes.float8_e5m2, 14)}[fmt]
    v = np.moveaxis(np.asarray(x, np.float32).astype(ml_dtypes.bfloat16).astype(np.float64), axis, -1)
    blocks = v.reshape(v.shape[:-1] + (-1, 32))
    amax = np.abs(blocks).max(-1, keepdims=True)
    byte = np.maximum(np.where(amax > 0, np.frexp(amax)[1] - 1 + 127, 0) - down, 1)
    scale = np.exp2(byte - 127.0)
    codes = (blocks / scale).astype(np.float32).astype(dtype).astype(np.float64)
    return np.moveaxis((codes * scale).reshape(v.shape), -1, axis)


WIDE = False


def mx_kscale(k):
    if not WIDE:
        return np.ones(k)
    levels = np.array([10, -10, 5, -5, 0])
    if k % 512:
        return np.exp2(np.random.permutation(np.resize(levels, k // 32))).repeat(32)
    a = np.empty((k // 512, 16))
    for p in range(k // 512):
        a[p, :8] = np.random.permutation(np.resize(levels, 8))
        for g in range(8):
            far = levels[np.abs(levels - a[p, g]) >= 10]
            a[p, g + 8] = far[np.random.randint(len(far))]
    return np.exp2(a.ravel()).repeat(32)


def f64(x):
    return np.asarray(x).astype(np.float64)


def striped(idx):
    return np.tile(idx.reshape(-1, 16).T, (8, 1)).astype(np.uint16)


def unstriped(offs):
    return offs[:16].T.reshape(-1).astype(np.int64)


def pack_weight(w):
    k, n = w.shape
    w = f64(np.asarray(w, np.float32).astype(ml_dtypes.bfloat16)).reshape(k // 32, 32, n)
    amax = np.abs(w).max(1)
    byte = np.clip(np.where(amax > 0, np.frexp(amax)[1] - 1 + 127 - 7, 1), 1, 254)
    scaled = (w * np.exp2(127.0 - byte)[:, None, :]).reshape(k, n).astype(np.float32)
    words = np.ascontiguousarray(scaled.reshape(k // 512, 128, 4, n).transpose(0, 1, 3, 2)).astype(ml_dtypes.float8_e4m3fn).view(np.uint8)
    return words, np.ascontiguousarray(byte.astype(np.uint8).reshape(k // 512, 16, n))


def unpack_weight(words, scales):
    g, p, n, _ = words.shape
    vals = np.ascontiguousarray(words).view(ml_dtypes.float8_e4m3fn).astype(np.float64) * np.repeat(np.exp2(scales.astype(np.float64) - 127.0), 8, axis=1)[..., None]
    return vals.transpose(0, 1, 3, 2).reshape(g * 512, n)


def relu(v):
    return np.maximum(v, 0.0)


def sigmoid(v):
    return 1.0 / (1.0 + np.exp(-np.maximum(v, -700.0)))

def planes(y):
    n, m = y.shape
    v = y.astype(np.float32).astype(ml_dtypes.bfloat16).astype(np.float64).reshape(n // 32, 32, m)
    top = np.abs(v).max(1)
    byte = np.clip(np.where(top > 0, np.frexp(top)[1] - 1 + 127 - 7, 1), 1, 254)
    codes = (v * np.exp2(127.0 - byte)[:, None, :]).reshape(n, m).astype(np.float32).astype(ml_dtypes.float8_e4m3fn).view(np.uint8)
    words = codes.reshape(n // 512, 128, 4, m).transpose(0, 1, 3, 2)
    return np.ascontiguousarray(words), np.ascontiguousarray(byte.astype(np.uint8).reshape(n // 512, 16, m))


K, T, N = 512, 512, 512


def setup_inputs():
    n = np.random.standard_normal
    s = mx_kscale(K)[:, None]
    packed_xT = pack_weight(n((K, T)) * s)
    return {
        "x_words": packed_xT[0],
        "x_scales": packed_xT[1],
        "w1": (n((K, N)) / np.sqrt(K) / s).astype(np.float32),
        "w2": (n((K, N)) / np.sqrt(K) / s).astype(np.float32),
        "w3": (n((K, N)) / np.sqrt(K) / s).astype(np.float32),
        "pos1": striped(np.random.permutation(T)),
        "pos2": striped(np.random.permutation(T)),
        "pos3": striped(np.random.permutation(T)),
        "pos4": striped(np.random.permutation(T)),
    }


def reference(x_words, x_scales, w1, w2, w3, pos1, pos2, pos3, pos4):
    xq = unpack_weight(x_words, x_scales)
    y = mxq(f64(w1), 0, "e4m3").T @ xq
    e = mxq(f64(w2), 0, "e4m3").T @ xq
    h = mxq(f64(w3), 0, "e4m3").T @ xq
    z = (sigmoid(y + e[:, unstriped(pos1)])) * h[:, unstriped(pos1)] + (sigmoid(y + e[:, unstriped(pos2)])) * h[:, unstriped(pos2)] + (sigmoid(y + e[:, unstriped(pos3)])) * h[:, unstriped(pos3)] + (sigmoid(y + e[:, unstriped(pos4)])) * h[:, unstriped(pos4)]
    out_0 = relu(z)
    return (out_0,) + planes(out_0)

@@ -1,0 +1,260 @@
+from contextlib import ExitStack
+
+import concourse.mybir as mybir
+from concourse.masks import make_identity
+
+K, T, N = 512, 512, 512
+FLOPS = 3 * 2 * K * T * N
+
+F32 = mybir.dt.float32
+BF16 = mybir.dt.bfloat16
+I32 = mybir.dt.int32
+U32 = mybir.dt.uint32
+U16 = mybir.dt.uint16
+U8 = mybir.dt.uint8
+FP8X4 = mybir.dt.float8_e4m3fn_x4
+ACT = mybir.ActivationFunctionType
+ALU = mybir.AluOpType
+
+P = 128
+PACK = 4
+TILES = N // P
+BLOCKS = T // P
+SPARE = 8
+PER_COLUMN = 16
+ORDER = ("e", "y", "h")
+HELD = 2
+HALVES = (slice(0, T // 2), slice(T // 2, T))
+LAST_TILE_CHUNKS = (256, 128, 128)
+
+
+def tile_picked_wgatedg_relu_lo_kernel(
+    tc, x_words, x_scales, w1, w2, w3, pos1, pos2, pos3, pos4, out_0, out_1, out_2
+):
+    nc = tc.nc
+    weights = {"y": w1, "e": w2, "h": w3}
+    lists_dram = (pos1, pos2, pos3, pos4)
+    D = len(lists_dram)
+
+    with ExitStack() as ctx:
+        keep = ctx.enter_context(tc.tile_pool(name="keep", bufs=1))
+        ring = ctx.enter_context(tc.tile_pool(name="ring", bufs=8))
+        small = ctx.enter_context(tc.tile_pool(name="small", bufs=3))
+        psum_acc = ctx.enter_context(tc.psum_pool(name="psum_acc", bufs=2))
+        psum = ctx.enter_context(tc.psum_pool(name="psum", bufs=3))
+
+        x_codes = keep.tile([P, T], U32, name="x_codes", align_bytes=64)
+        x_scale = keep.tile([P, T], U8, name="x_scale", align_bytes=64)
+        lists = [keep.tile([P, T // PER_COLUMN], U16, name="list%d" % d) for d in range(D)]
+        raw_first = {n: keep.tile([P, PACK, P], F32, name="raw_first_" + n) for n in weights}
+        raw_second = {n: keep.tile([P, PACK, P], F32, name="raw_second_" + n) for n in weights}
+        raw_rest = {n: keep.tile([P, PACK, N - 2 * P], F32, name="raw_rest_" + n) for n in weights}
+        rows = {n: w.rearrange("(p j) c -> p j c", j=PACK) for n, w in weights.items()}
+
+        warm = keep.tile([P, 1], F32, name="warm")
+        nc.vector.memset(x_scale[:].bitcast(I32), 0)
+        nc.vector.memset(warm[:], 0.0)
+        nc.scalar.activation(warm[:], warm[:], ACT.Sigmoid)
+
+        nc.sync.dma_start(out=raw_first["e"][:], in_=rows["e"][:, :, 0:P])
+        nc.sync.dma_start(out=raw_first["y"][:], in_=rows["y"][:, :, 0:P])
+        for q in range(4):
+            nc.sync.dma_start(
+                out=x_scale[32 * q : 32 * q + 4, :].bitcast(I32),
+                in_=x_scales[0, 4 * q : 4 * q + 4, :].bitcast(I32),
+            )
+        x_rows = x_words[0].rearrange("p c r -> p (c r)").bitcast(I32)
+        for half in HALVES:
+            nc.sync.dma_start(out=x_codes[:, half].bitcast(I32), in_=x_rows[:, half])
+        nc.sync.dma_start(lists[0][:], lists_dram[0])
+        nc.sync.dma_start(out=raw_first["h"][:], in_=rows["h"][:, :, 0:P])
+        for d in range(1, D):
+            nc.sync.dma_start(lists[d][:], lists_dram[d])
+        for n in ORDER:
+            nc.sync.dma_start(out=raw_second[n][:], in_=rows[n][:, :, P : 2 * P])
+        for n in ORDER:
+            nc.sync.dma_start(out=raw_rest[n][:], in_=rows[n][:, :, 2 * P : N])
+
+        ident = keep.tile([P, P], F32, name="ident")
+        make_identity(nc, ident[:])
+
+        result = {}
+        for j in range(TILES):
+            for n in ("e", "h"):
+                result[n, j] = keep.tile([P, T + SPARE], F32, name="%s%d" % (n, j))
+                nc.gpsimd.memset(result[n, j][:, T:], 0.0)
+            result["y", j] = keep.tile([P, T], F32, name="y%d" % j)
+
+        pairs = keep.tile([P, BLOCKS, 2, P, 2], BF16, name="pairs")
+        out_codes = keep.tile([P, T], U32, name="out_codes", align_bytes=64)
+        out_scale = keep.tile([P, T], U8, name="out_scale", align_bytes=64)
+
+        def cast(engine_copy, dst, raw):
+            engine_copy(
+                out=dst.rearrange("p (c i) t -> p c t i", i=4),
+                in_=raw.rearrange("p t (c i) -> p c t i", i=4),
+            )
+
+        def multiply(n, j, codes, scale, engine_copy, cols, acc):
+            nc.tensor.matmul_mx(
+                out=acc[:],
+                lhsT=codes.bitcast(FP8X4),
+                lhsT_scale=scale,
+                rhs=x_codes[:, cols].bitcast(FP8X4),
+                rhs_scale=x_scale[:, cols],
+                start=True,
+                stop=True,
+            )
+            engine_copy(out=result[n, j][:, cols], in_=acc[:])
+
+        def quantise_first(n, on_vector):
+            grouped = small.tile([P, P, PACK], BF16, name="grouped", align_bytes=64)
+            if on_vector:
+                cast(nc.vector.tensor_copy, grouped[:, 0:on_vector, :], raw_first[n][:, :, 0:on_vector])
+            cast(nc.scalar.copy, grouped[:, on_vector:P, :], raw_first[n][:, :, on_vector:P])
+            codes = small.tile([P, P], U32, name="codes", align_bytes=64)
+            scale = small.tile([P, P], U8, name="scale", align_bytes=64)
+            nc.vector.quantize_mx(
+                out=codes[:].bitcast(FP8X4), scales=scale[:], in_=grouped[:].rearrange("p c t -> p (c t)")
+            )
+            return codes[:], scale[:]
+
+        def project(j):
+            grouped = keep.tile([P, 3 * P, PACK], BF16, name="grouped%d" % j, tag="held%d" % j, align_bytes=64)
+            for i, n in enumerate(ORDER):
+                raw = raw_second[n][:] if j == 1 else raw_rest[n][:, :, (j - 2) * P : (j - 1) * P]
+                cast(nc.scalar.copy, grouped[:, i * P : (i + 1) * P, :], raw)
+            codes = keep.tile([P, 3 * P], U32, name="codes%d" % j, align_bytes=64)
+            scale = keep.tile([P, 3 * P], U8, name="scale%d" % j, align_bytes=64)
+            for cols in (slice(0, 2 * P), slice(2 * P, 3 * P)):
+                nc.vector.quantize_mx(
+                    out=codes[:, cols].bitcast(FP8X4),
+                    scales=scale[:, cols],
+                    in_=grouped[:, cols, :].rearrange("p c t -> p (c t)"),
+                )
+            for i, n in enumerate(ORDER):
+                cols = slice(i * P, (i + 1) * P)
+                acc = psum_acc.tile([P, T], F32, name="acc")
+                multiply(n, j, codes[:, cols], scale[:, cols], nc.scalar.copy, slice(0, T), acc)
+
+        def offsets(d, v0, width):
+            return lists[d][:, v0 // PER_COLUMN : (v0 + width) // PER_COLUMN]
+
+        def gates(j, v0, width):
+            made = []
+            for d in range(D):
+                pre = ring.tile([P, width], F32, name="pre")
+                nc.vector.tensor_tensor(
+                    pre[:], result["e", j][:].indirect(offsets(d, v0, width)), result["y", j][:, v0 : v0 + width], ALU.add
+                )
+                gate = ring.tile([P, width], F32, name="gate")
+                nc.scalar.activation(gate[:], pre[:], ACT.Sigmoid)
+                made.append(gate)
+            return made
+
+        def messages(j, v0, width, gate):
+            made = []
+            for d in range(D):
+                if d == HELD and j + 1 < TILES:
+                    msg = keep.tile([P, width], F32, name="msg_held%d" % j, tag="held%d" % (j + 1), align_bytes=64)
+                else:
+                    msg = ring.tile([P, width], F32, name="msg")
+                nc.vector.tensor_tensor(
+                    msg[:], result["h", j][:].indirect(offsets(d, v0, width)), gate[d][:, v0 : v0 + width], ALU.mult
+                )
+                made.append(msg)
+            return made
+
+        def add_block(total, msg, b):
+            for d in range(D):
+                nc.tensor.matmul(
+                    total, msg[d][:, b * P : (b + 1) * P], ident[:],
+                    start=(d == 0), stop=(d == D - 1), is_transpose=True,
+                )
+
+        def pair_columns(j):
+            return slice(j * P // PACK, (j + 1) * P // PACK)
+
+        def finish_tile(j, msg):
+            total = psum.tile([P, BLOCKS, P], F32, name="total")
+            for b in range(BLOCKS):
+                add_block(total[:, b, :], msg, b)
+            z_t = small.tile([P, BLOCKS, P], F32, name="z_t")
+            nc.scalar.activation(z_t[:], total[:], ACT.Relu)
+            nc.scalar.copy(
+                out=pairs[:, :, :, pair_columns(j), :],
+                in_=z_t[:].rearrange("v b (q u e) -> v b u q e", u=2, e=2),
+            )
+            back = psum.tile([P, BLOCKS, P], F32, name="back")
+            for b in range(BLOCKS):
+                nc.tensor.transpose(back[:, b, :], z_t[:, b, :], ident[:])
+            staged = small.tile([P, T], F32, name="staged")
+            nc.scalar.copy(out=staged[:], in_=back[:].rearrange("m b v -> m (b v)"))
+            nc.sync.dma_start(out=out_0[j * P : (j + 1) * P, :], in_=staged[:])
+
+        out_words = out_1[0].rearrange("p c r -> p (c r)").bitcast(I32)
+
+        def finish_block(j, msg, b_local, b, word_copy):
+            cols = slice(b * P, (b + 1) * P)
+            total = psum.tile([P, P], F32, name="total")
+            add_block(total[:], msg, b_local)
+            nc.scalar.activation(
+                pairs[:, b, :, pair_columns(j), :],
+                total[:].rearrange("v (q u e) -> v u q e", u=2, e=2),
+                ACT.Relu,
+            )
+            z_t = keep.tile([P, P], F32, name="z_last%d" % b)
+            nc.scalar.activation(z_t[:], total[:], ACT.Relu)
+            words = psum.tile([P, 2, P], F32, name="words", tag="back")
+            for u in range(2):
+                nc.tensor.transpose(
+                    words[:, u, :], pairs[:, b, u, :, :].rearrange("v p e -> v (p e)").bitcast(F32), ident[:]
+                )
+            back = psum.tile([P, P], F32, name="back")
+            nc.tensor.transpose(back[:], z_t[:], ident[:])
+            rounded = keep.tile([P, P, PACK], BF16, name="rounded%d" % b, align_bytes=64)
+            word_copy(out=rounded[:].bitcast(F32), in_=words[:].rearrange("p u v -> p v u"))
+            staged = keep.tile([P, P], F32, name="staged%d" % b)
+            nc.scalar.copy(out=staged[:], in_=back[:])
+            nc.sync.dma_start(out=out_0[j * P : (j + 1) * P, cols], in_=staged[:])
+            nc.vector.quantize_mx(
+                out=out_codes[:, cols].bitcast(FP8X4),
+                scales=out_scale[:, cols],
+                in_=rounded[:].rearrange("p v t -> p (v t)"),
+            )
+            nc.sync.dma_start(out=out_words[:, cols], in_=out_codes[:, cols].bitcast(I32))
+
+        first_e = quantise_first("e", 80)
+        first_y = quantise_first("y", 80)
+        for half in HALVES:
+            acc = psum_acc.tile([P, T // 2], F32, name="acc")
+            multiply("e", 0, *first_e, nc.scalar.copy, half, acc)
+            acc = psum.tile([P, T // 2], F32, name="total")
+            multiply("y", 0, *first_y, nc.vector.tensor_copy, half, acc)
+        for j in range(TILES - 1):
+            if j > 0:
+                project(j + 1)
+            gate = gates(j, 0, T)
+            if j == 0:
+                first_h = quantise_first("h", 0)
+                acc = psum_acc.tile([P, T], F32, name="acc")
+                multiply("h", 0, *first_h, nc.scalar.copy, slice(0, T), acc)
+                project(j + 1)
+            msg = messages(j, 0, T, gate)
+            finish_tile(j, msg)
+
+        j = TILES - 1
+        v0 = 0
+        gate = gates(j, 0, T)
+        for c, width in enumerate(LAST_TILE_CHUNKS):
+            last = c == len(LAST_TILE_CHUNKS) - 1
+            msg = messages(j, v0, width, gate)
+            for b_local in range(width // P):
+                finish_block(j, msg, b_local, v0 // P + b_local, nc.vector.tensor_copy if last else nc.scalar.copy)
+            v0 = v0 + width
+        for q in range(4):
+            queue = nc.sync if q % 2 == 0 else nc.scalar
+            queue.dma_start(
+                out=out_2[0, 4 * q : 4 * q + 4, :].bitcast(I32),
+                in_=out_scale[32 * q : 32 * q + 4, :].bitcast(I32),
+            )

@@ -25,7 +25,7 @@ PER_COLUMN = 16
 ORDER = ("e", "y", "h")
 HELD = 2
 HALVES = (slice(0, T // 2), slice(T // 2, T))
-LAST_TILE_CHUNKS = (256, 128, 128)
+LAST_TILE_CHUNKS = (128, 128, 128, 128)
 
 
 def tile_picked_wgatedg_relu_lo_kernel(
@@ -82,11 +82,9 @@ def tile_picked_wgatedg_relu_lo_kernel(
         for j in range(TILES):
             for n in ("e", "h"):
                 result[n, j] = keep.tile([P, T + SPARE], F32, name="%s%d" % (n, j))
-                nc.gpsimd.memset(result[n, j][:, T:], 0.0)
             result["y", j] = keep.tile([P, T], F32, name="y%d" % j)
 
         pairs = keep.tile([P, BLOCKS, 2, P, 2], BF16, name="pairs")
-        out_codes = keep.tile([P, T], U32, name="out_codes", align_bytes=64)
         out_scale = keep.tile([P, T], U8, name="out_scale", align_bytes=64)
 
         def cast(engine_copy, dst, raw):
@@ -107,11 +105,14 @@ def tile_picked_wgatedg_relu_lo_kernel(
             )
             engine_copy(out=result[n, j][:, cols], in_=acc[:])
 
-        def quantise_first(n, on_vector):
+        def round_first(n, on_vector):
             grouped = small.tile([P, P, PACK], BF16, name="grouped", align_bytes=64)
             if on_vector:
                 cast(nc.vector.tensor_copy, grouped[:, 0:on_vector, :], raw_first[n][:, :, 0:on_vector])
             cast(nc.scalar.copy, grouped[:, on_vector:P, :], raw_first[n][:, :, on_vector:P])
+            return grouped
+
+        def quantise_first(grouped):
             codes = small.tile([P, P], U32, name="codes", align_bytes=64)
             scale = small.tile([P, P], U8, name="scale", align_bytes=64)
             nc.vector.quantize_mx(
@@ -119,11 +120,14 @@ def tile_picked_wgatedg_relu_lo_kernel(
             )
             return codes[:], scale[:]
 
-        def project(j):
+        def round_tile(j):
             grouped = keep.tile([P, 3 * P, PACK], BF16, name="grouped%d" % j, tag="held%d" % j, align_bytes=64)
             for i, n in enumerate(ORDER):
                 raw = raw_second[n][:] if j == 1 else raw_rest[n][:, :, (j - 2) * P : (j - 1) * P]
                 cast(nc.scalar.copy, grouped[:, i * P : (i + 1) * P, :], raw)
+            return grouped
+
+        def project(j, grouped):
             codes = keep.tile([P, 3 * P], U32, name="codes%d" % j, align_bytes=64)
             scale = keep.tile([P, 3 * P], U8, name="scale%d" % j, align_bytes=64)
             for cols in (slice(0, 2 * P), slice(2 * P, 3 * P)):
@@ -144,10 +148,17 @@ def tile_picked_wgatedg_relu_lo_kernel(
             made = []
             for d in range(D):
                 pre = ring.tile([P, width], F32, name="pre")
-                nc.vector.tensor_tensor(
-                    pre[:], result["e", j][:].indirect(offsets(d, v0, width)), result["y", j][:, v0 : v0 + width], ALU.add
-                )
-                gate = ring.tile([P, width], F32, name="gate")
+                for part in HALVES if (j, d) == (0, 0) else (slice(0, T),):
+                    nc.vector.tensor_tensor(
+                        pre[:, part],
+                        result["e", j][:].indirect(offsets(d, part.start, part.stop - part.start)),
+                        result["y", j][:, part],
+                        ALU.add,
+                    )
+                if j == TILES - 1 and d == D - 1:
+                    gate = keep.tile([P, width], F32, name="last_gate", tag="late", align_bytes=64)
+                else:
+                    gate = ring.tile([P, width], F32, name="gate")
                 nc.scalar.activation(gate[:], pre[:], ACT.Sigmoid)
                 made.append(gate)
             return made
@@ -157,6 +168,8 @@ def tile_picked_wgatedg_relu_lo_kernel(
             for d in range(D):
                 if d == HELD and j + 1 < TILES:
                     msg = keep.tile([P, width], F32, name="msg_held%d" % j, tag="held%d" % (j + 1), align_bytes=64)
+                elif d == HELD and v0 == T - P:
+                    msg = keep.tile([P, width], F32, name="msg_last", tag="z_last1")
                 else:
                     msg = ring.tile([P, width], F32, name="msg")
                 nc.vector.tensor_tensor(
@@ -175,12 +188,15 @@ def tile_picked_wgatedg_relu_lo_kernel(
         def pair_columns(j):
             return slice(j * P // PACK, (j + 1) * P // PACK)
 
-        def finish_tile(j, msg):
+        def sum_tile(msg):
             total = psum.tile([P, BLOCKS, P], F32, name="total")
             for b in range(BLOCKS):
                 add_block(total[:, b, :], msg, b)
             z_t = small.tile([P, BLOCKS, P], F32, name="z_t")
             nc.scalar.activation(z_t[:], total[:], ACT.Relu)
+            return z_t
+
+        def finish_tile(j, z_t):
             nc.scalar.copy(
                 out=pairs[:, :, :, pair_columns(j), :],
                 in_=z_t[:].rearrange("v b (q u e) -> v b u q e", u=2, e=2),
@@ -203,9 +219,9 @@ def tile_picked_wgatedg_relu_lo_kernel(
                 total[:].rearrange("v (q u e) -> v u q e", u=2, e=2),
                 ACT.Relu,
             )
-            z_t = keep.tile([P, P], F32, name="z_last%d" % b)
+            z_t = keep.tile([P, P], F32, name="z_last%d" % b, tag="z_last%d" % b)
             nc.scalar.activation(z_t[:], total[:], ACT.Relu)
-            words = psum.tile([P, 2, P], F32, name="words", tag="back")
+            words = psum_acc.tile([P, 2, P], F32, name="words", tag="acc")
             for u in range(2):
                 nc.tensor.transpose(
                     words[:, u, :], pairs[:, b, u, :, :].rearrange("v p e -> v (p e)").bitcast(F32), ident[:]
@@ -217,41 +233,51 @@ def tile_picked_wgatedg_relu_lo_kernel(
             staged = keep.tile([P, P], F32, name="staged%d" % b)
             nc.scalar.copy(out=staged[:], in_=back[:])
             nc.sync.dma_start(out=out_0[j * P : (j + 1) * P, cols], in_=staged[:])
-            nc.vector.quantize_mx(
-                out=out_codes[:, cols].bitcast(FP8X4),
-                scales=out_scale[:, cols],
-                in_=rounded[:].rearrange("p v t -> p (v t)"),
-            )
-            nc.sync.dma_start(out=out_words[:, cols], in_=out_codes[:, cols].bitcast(I32))
+            return rounded
 
-        first_e = quantise_first("e", 80)
-        first_y = quantise_first("y", 80)
+        first_e = quantise_first(round_first("e", 80))
+        first_y = quantise_first(round_first("y", 80))
         for half in HALVES:
             acc = psum_acc.tile([P, T // 2], F32, name="acc")
             multiply("e", 0, *first_e, nc.scalar.copy, half, acc)
+        for half, engine_copy in zip(HALVES, (nc.vector.tensor_copy, nc.scalar.copy)):
             acc = psum.tile([P, T // 2], F32, name="total")
-            multiply("y", 0, *first_y, nc.vector.tensor_copy, half, acc)
+            multiply("y", 0, *first_y, engine_copy, half, acc)
+        first_h = quantise_first(round_first("h", 0))
+        acc = psum_acc.tile([P, T], F32, name="acc")
+        multiply("h", 0, *first_h, nc.scalar.copy, slice(0, T), acc)
         for j in range(TILES - 1):
-            if j > 0:
-                project(j + 1)
+            grouped = round_tile(j + 1)
             gate = gates(j, 0, T)
-            if j == 0:
-                first_h = quantise_first("h", 0)
-                acc = psum_acc.tile([P, T], F32, name="acc")
-                multiply("h", 0, *first_h, nc.scalar.copy, slice(0, T), acc)
-                project(j + 1)
+            project(j + 1, grouped)
+            if j > 0:
+                finish_tile(j - 1, sum_tile(msg))
             msg = messages(j, 0, T, gate)
-            finish_tile(j, msg)
 
         j = TILES - 1
         v0 = 0
+        rounded = []
+        z_t = sum_tile(msg)
         gate = gates(j, 0, T)
+        finish_tile(j - 1, z_t)
         for c, width in enumerate(LAST_TILE_CHUNKS):
             last = c == len(LAST_TILE_CHUNKS) - 1
             msg = messages(j, v0, width, gate)
             for b_local in range(width // P):
-                finish_block(j, msg, b_local, v0 // P + b_local, nc.vector.tensor_copy if last else nc.scalar.copy)
+                rounded.append(
+                    finish_block(j, msg, b_local, v0 // P + b_local, nc.vector.tensor_copy if last else nc.scalar.copy)
+                )
             v0 = v0 + width
+        out_codes = keep.tile([P, T], U32, name="out_codes", tag="late", align_bytes=64)
+        for b in range(BLOCKS):
+            cols = slice(b * P, (b + 1) * P)
+            nc.vector.quantize_mx(
+                out=out_codes[:, cols].bitcast(FP8X4),
+                scales=out_scale[:, cols],
+                in_=rounded[b][:].rearrange("p v t -> p (v t)"),
+            )
+        for cols in (slice(0, T - P), slice(T - P, T)):
+            nc.sync.dma_start(out=out_words[:, cols], in_=out_codes[:, cols].bitcast(I32))
         for q in range(4):
             queue = nc.sync if q % 2 == 0 else nc.scalar
             queue.dma_start(

@@ -41,7 +41,7 @@ def tile_picked_wgatedg_relu_lo_kernel(
         ring = ctx.enter_context(tc.tile_pool(name="ring", bufs=8))
         small = ctx.enter_context(tc.tile_pool(name="small", bufs=3))
         psum_acc = ctx.enter_context(tc.psum_pool(name="psum_acc", bufs=2))
-        psum = ctx.enter_context(tc.psum_pool(name="psum", bufs=3))
+        psum = ctx.enter_context(tc.psum_pool(name="psum", bufs=2))
 
         x_codes = keep.tile([P, T], U32, name="x_codes", align_bytes=64)
         x_scale = keep.tile([P, T], U8, name="x_scale", align_bytes=64)
@@ -168,8 +168,6 @@ def tile_picked_wgatedg_relu_lo_kernel(
             for d in range(D):
                 if d == HELD and j + 1 < TILES:
                     msg = keep.tile([P, width], F32, name="msg_held%d" % j, tag="held%d" % (j + 1), align_bytes=64)
-                elif d == HELD and v0 == T - P:
-                    msg = keep.tile([P, width], F32, name="msg_last", tag="z_last1")
                 else:
                     msg = ring.tile([P, width], F32, name="msg")
                 nc.vector.tensor_tensor(
@@ -219,7 +217,7 @@ def tile_picked_wgatedg_relu_lo_kernel(
                 total[:].rearrange("v (q u e) -> v u q e", u=2, e=2),
                 ACT.Relu,
             )
-            z_t = keep.tile([P, P], F32, name="z_last%d" % b, tag="z_last%d" % b)
+            z_t = keep.tile([P, P], F32, name="z_last%d" % b)
             nc.scalar.activation(z_t[:], total[:], ACT.Relu)
             words = psum_acc.tile([P, 2, P], F32, name="words", tag="acc")
             for u in range(2):

from contextlib import ExitStack

import concourse.mybir as mybir
from concourse.masks import make_identity

K, T, N = 512, 512, 512
FLOPS = 3 * 2 * K * T * N

F32 = mybir.dt.float32
BF16 = mybir.dt.bfloat16
I32 = mybir.dt.int32
U32 = mybir.dt.uint32
U16 = mybir.dt.uint16
U8 = mybir.dt.uint8
FP8X4 = mybir.dt.float8_e4m3fn_x4
ACT = mybir.ActivationFunctionType
ALU = mybir.AluOpType

P = 128
PACK = 4
TILES = N // P
BLOCKS = T // P
SPARE = 8
PER_COLUMN = 16
ORDER = ("e", "y", "h")
HELD = 2
HALVES = (slice(0, T // 2), slice(T // 2, T))
LAST_TILE_CHUNKS = (128, 128, 128, 128)


def tile_picked_wgatedg_relu_lo_kernel(
    tc, x_words, x_scales, w1, w2, w3, pos1, pos2, pos3, pos4, out_0, out_1, out_2
):
    nc = tc.nc
    weights = {"y": w1, "e": w2, "h": w3}
    lists_dram = (pos1, pos2, pos3, pos4)
    D = len(lists_dram)

    with ExitStack() as ctx:
        keep = ctx.enter_context(tc.tile_pool(name="keep", bufs=1))
        ring = ctx.enter_context(tc.tile_pool(name="ring", bufs=8))
        small = ctx.enter_context(tc.tile_pool(name="small", bufs=3))
        psum_acc = ctx.enter_context(tc.psum_pool(name="psum_acc", bufs=2))
        psum = ctx.enter_context(tc.psum_pool(name="psum", bufs=2))

        x_codes = keep.tile([P, T], U32, name="x_codes", align_bytes=64)
        x_scale = keep.tile([P, T], U8, name="x_scale", align_bytes=64)
        lists = [keep.tile([P, T // PER_COLUMN], U16, name="list%d" % d) for d in range(D)]
        raw_first = {n: keep.tile([P, PACK, P], F32, name="raw_first_" + n) for n in weights}
        raw_second = {n: keep.tile([P, PACK, P], F32, name="raw_second_" + n) for n in weights}
        raw_rest = {n: keep.tile([P, PACK, N - 2 * P], F32, name="raw_rest_" + n) for n in weights}
        rows = {n: w.rearrange("(p j) c -> p j c", j=PACK) for n, w in weights.items()}

        warm = keep.tile([P, 1], F32, name="warm")
        nc.vector.memset(x_scale[:].bitcast(I32), 0)
        nc.vector.memset(warm[:], 0.0)
        nc.scalar.activation(warm[:], warm[:], ACT.Sigmoid)

        nc.sync.dma_start(out=raw_first["e"][:], in_=rows["e"][:, :, 0:P])
        nc.sync.dma_start(out=raw_first["y"][:], in_=rows["y"][:, :, 0:P])
        for q in range(4):
            nc.sync.dma_start(
                out=x_scale[32 * q : 32 * q + 4, :].bitcast(I32),
                in_=x_scales[0, 4 * q : 4 * q + 4, :].bitcast(I32),
            )
        x_rows = x_words[0].rearrange("p c r -> p (c r)").bitcast(I32)
        for half in HALVES:
            nc.sync.dma_start(out=x_codes[:, half].bitcast(I32), in_=x_rows[:, half])
        nc.sync.dma_start(lists[0][:], lists_dram[0])
        nc.sync.dma_start(out=raw_first["h"][:], in_=rows["h"][:, :, 0:P])
        for d in range(1, D):
            nc.sync.dma_start(lists[d][:], lists_dram[d])
        for n in ORDER:
            nc.sync.dma_start(out=raw_second[n][:], in_=rows[n][:, :, P : 2 * P])
        for n in ORDER:
            nc.sync.dma_start(out=raw_rest[n][:], in_=rows[n][:, :, 2 * P : N])

        ident = keep.tile([P, P], F32, name="ident")
        make_identity(nc, ident[:])

        result = {}
        for j in range(TILES):
            for n in ("e", "h"):
                result[n, j] = keep.tile([P, T + SPARE], F32, name="%s%d" % (n, j))
            result["y", j] = keep.tile([P, T], F32, name="y%d" % j)

        pairs = keep.tile([P, BLOCKS, 2, P, 2], BF16, name="pairs")
        out_scale = keep.tile([P, T], U8, name="out_scale", align_bytes=64)

        def cast(engine_copy, dst, raw):
            engine_copy(
                out=dst.rearrange("p (c i) t -> p c t i", i=4),
                in_=raw.rearrange("p t (c i) -> p c t i", i=4),
            )

        def multiply(n, j, codes, scale, engine_copy, cols, acc):
            nc.tensor.matmul_mx(
                out=acc[:],
                lhsT=codes.bitcast(FP8X4),
                lhsT_scale=scale,
                rhs=x_codes[:, cols].bitcast(FP8X4),
                rhs_scale=x_scale[:, cols],
                start=True,
                stop=True,
            )
            engine_copy(out=result[n, j][:, cols], in_=acc[:])

        def round_first(n, on_vector):
            grouped = small.tile([P, P, PACK], BF16, name="grouped", align_bytes=64)
            if on_vector:
                cast(nc.vector.tensor_copy, grouped[:, 0:on_vector, :], raw_first[n][:, :, 0:on_vector])
            cast(nc.scalar.copy, grouped[:, on_vector:P, :], raw_first[n][:, :, on_vector:P])
            return grouped

        def quantise_first(grouped):
            codes = small.tile([P, P], U32, name="codes", align_bytes=64)
            scale = small.tile([P, P], U8, name="scale", align_bytes=64)
            nc.vector.quantize_mx(
                out=codes[:].bitcast(FP8X4), scales=scale[:], in_=grouped[:].rearrange("p c t -> p (c t)")
            )
            return codes[:], scale[:]

        def round_tile(j):
            grouped = keep.tile([P, 3 * P, PACK], BF16, name="grouped%d" % j, tag="held%d" % j, align_bytes=64)
            for i, n in enumerate(ORDER):
                raw = raw_second[n][:] if j == 1 else raw_rest[n][:, :, (j - 2) * P : (j - 1) * P]
                cast(nc.scalar.copy, grouped[:, i * P : (i + 1) * P, :], raw)
            return grouped

        def project(j, grouped):
            codes = keep.tile([P, 3 * P], U32, name="codes%d" % j, align_bytes=64)
            scale = keep.tile([P, 3 * P], U8, name="scale%d" % j, align_bytes=64)
            for cols in (slice(0, 2 * P), slice(2 * P, 3 * P)):
                nc.vector.quantize_mx(
                    out=codes[:, cols].bitcast(FP8X4),
                    scales=scale[:, cols],
                    in_=grouped[:, cols, :].rearrange("p c t -> p (c t)"),
                )
            for i, n in enumerate(ORDER):
                cols = slice(i * P, (i + 1) * P)
                acc = psum_acc.tile([P, T], F32, name="acc")
                multiply(n, j, codes[:, cols], scale[:, cols], nc.scalar.copy, slice(0, T), acc)

        def offsets(d, v0, width):
            return lists[d][:, v0 // PER_COLUMN : (v0 + width) // PER_COLUMN]

        def gates(j, v0, width):
            made = []
            for d in range(D):
                pre = ring.tile([P, width], F32, name="pre")
                for part in HALVES if (j, d) == (0, 0) else (slice(0, T),):
                    nc.vector.tensor_tensor(
                        pre[:, part],
                        result["e", j][:].indirect(offsets(d, part.start, part.stop - part.start)),
                        result["y", j][:, part],
                        ALU.add,
                    )
                if j == TILES - 1 and d == D - 1:
                    gate = keep.tile([P, width], F32, name="last_gate", tag="late", align_bytes=64)
                else:
                    gate = ring.tile([P, width], F32, name="gate")
                nc.scalar.activation(gate[:], pre[:], ACT.Sigmoid)
                made.append(gate)
            return made

        def messages(j, v0, width, gate):
            made = []
            for d in range(D):
                if d == HELD and j + 1 < TILES:
                    msg = keep.tile([P, width], F32, name="msg_held%d" % j, tag="held%d" % (j + 1), align_bytes=64)
                else:
                    msg = ring.tile([P, width], F32, name="msg")
                nc.vector.tensor_tensor(
                    msg[:], result["h", j][:].indirect(offsets(d, v0, width)), gate[d][:, v0 : v0 + width], ALU.mult
                )
                made.append(msg)
            return made

        def add_block(total, msg, b):
            for d in range(D):
                nc.tensor.matmul(
                    total, msg[d][:, b * P : (b + 1) * P], ident[:],
                    start=(d == 0), stop=(d == D - 1), is_transpose=True,
                )

        def pair_columns(j):
            return slice(j * P // PACK, (j + 1) * P // PACK)

        def sum_tile(msg):
            total = psum.tile([P, BLOCKS, P], F32, name="total")
            for b in range(BLOCKS):
                add_block(total[:, b, :], msg, b)
            z_t = small.tile([P, BLOCKS, P], F32, name="z_t")
            nc.scalar.activation(z_t[:], total[:], ACT.Relu)
            return z_t

        def finish_tile(j, z_t):
            nc.scalar.copy(
                out=pairs[:, :, :, pair_columns(j), :],
                in_=z_t[:].rearrange("v b (q u e) -> v b u q e", u=2, e=2),
            )
            back = psum.tile([P, BLOCKS, P], F32, name="back")
            for b in range(BLOCKS):
                nc.tensor.transpose(back[:, b, :], z_t[:, b, :], ident[:])
            staged = small.tile([P, T], F32, name="staged")
            nc.scalar.copy(out=staged[:], in_=back[:].rearrange("m b v -> m (b v)"))
            nc.sync.dma_start(out=out_0[j * P : (j + 1) * P, :], in_=staged[:])

        out_words = out_1[0].rearrange("p c r -> p (c r)").bitcast(I32)

        def finish_block(j, msg, b_local, b, word_copy):
            cols = slice(b * P, (b + 1) * P)
            total = psum.tile([P, P], F32, name="total")
            add_block(total[:], msg, b_local)
            nc.scalar.activation(
                pairs[:, b, :, pair_columns(j), :],
                total[:].rearrange("v (q u e) -> v u q e", u=2, e=2),
                ACT.Relu,
            )
            z_t = keep.tile([P, P], F32, name="z_last%d" % b)
            nc.scalar.activation(z_t[:], total[:], ACT.Relu)
            words = psum_acc.tile([P, 2, P], F32, name="words", tag="acc")
            for u in range(2):
                nc.tensor.transpose(
                    words[:, u, :], pairs[:, b, u, :, :].rearrange("v p e -> v (p e)").bitcast(F32), ident[:]
                )
            back = psum.tile([P, P], F32, name="back")
            nc.tensor.transpose(back[:], z_t[:], ident[:])
            rounded = keep.tile([P, P, PACK], BF16, name="rounded%d" % b, align_bytes=64)
            word_copy(out=rounded[:].bitcast(F32), in_=words[:].rearrange("p u v -> p v u"))
            staged = keep.tile([P, P], F32, name="staged%d" % b)
            nc.scalar.copy(out=staged[:], in_=back[:])
            nc.sync.dma_start(out=out_0[j * P : (j + 1) * P, cols], in_=staged[:])
            return rounded

        first_e = quantise_first(round_first("e", 80))
        first_y = quantise_first(round_first("y", 80))
        for half in HALVES:
            acc = psum_acc.tile([P, T // 2], F32, name="acc")
            multiply("e", 0, *first_e, nc.scalar.copy, half, acc)
        for half, engine_copy in zip(HALVES, (nc.vector.tensor_copy, nc.scalar.copy)):
            acc = psum.tile([P, T // 2], F32, name="total")
            multiply("y", 0, *first_y, engine_copy, half, acc)
        first_h = quantise_first(round_first("h", 0))
        acc = psum_acc.tile([P, T], F32, name="acc")
        multiply("h", 0, *first_h, nc.scalar.copy, slice(0, T), acc)
        for j in range(TILES - 1):
            grouped = round_tile(j + 1)
            gate = gates(j, 0, T)
            project(j + 1, grouped)
            if j > 0:
                finish_tile(j - 1, sum_tile(msg))
            msg = messages(j, 0, T, gate)

        j = TILES - 1
        v0 = 0
        rounded = []
        z_t = sum_tile(msg)
        gate = gates(j, 0, T)
        finish_tile(j - 1, z_t)
        for c, width in enumerate(LAST_TILE_CHUNKS):
            last = c == len(LAST_TILE_CHUNKS) - 1
            msg = messages(j, v0, width, gate)
            for b_local in range(width // P):
                rounded.append(
                    finish_block(j, msg, b_local, v0 // P + b_local, nc.vector.tensor_copy if last else nc.scalar.copy)
                )
            v0 = v0 + width
        out_codes = keep.tile([P, T], U32, name="out_codes", tag="late", align_bytes=64)
        for b in range(BLOCKS):
            cols = slice(b * P, (b + 1) * P)
            nc.vector.quantize_mx(
                out=out_codes[:, cols].bitcast(FP8X4),
                scales=out_scale[:, cols],
                in_=rounded[b][:].rearrange("p v t -> p (v t)"),
            )
        for cols in (slice(0, T - P), slice(T - P, T)):
            nc.sync.dma_start(out=out_words[:, cols], in_=out_codes[:, cols].bitcast(I32))
        for q in range(4):
            queue = nc.sync if q % 2 == 0 else nc.scalar
            queue.dma_start(
                out=out_2[0, 4 * q : 4 * q + 4, :].bitcast(I32),
                in_=out_scale[32 * q : 32 * q + 4, :].bitcast(I32),
            )
